import numpy as np
import ml_dtypes


def mxq(x, axis, fmt="e4m3"):
    dtype, down = {"e4m3": (ml_dtypes.float8_e4m3fn, 7), "e5m2": (ml_dtypes.float8_e5m2, 14)}[fmt]
    v = np.moveaxis(np.asarray(x, np.float32).astype(ml_dtypes.bfloat16).astype(np.float64), axis, -1)
    blocks = v.reshape(v.shape[:-1] + (-1, 32))
    amax = np.abs(blocks).max(-1, keepdims=True)
    byte = np.maximum(np.where(amax > 0, np.frexp(amax)[1] - 1 + 127, 0) - down, 1)
    scale = np.exp2(byte - 127.0)
    codes = (blocks / scale).astype(np.float32).astype(dtype).astype(np.float64)
    return np.moveaxis((codes * scale).reshape(v.shape), -1, axis)


WIDE = False


def mx_kscale(k):
    if not WIDE:
        return np.ones(k)
    levels = np.array([10, -10, 5, -5, 0])
    if k % 512:
        return np.exp2(np.random.permutation(np.resize(levels, k // 32))).repeat(32)
    a = np.empty((k // 512, 16))
    for p in range(k // 512):
        a[p, :8] = np.random.permutation(np.resize(levels, 8))
        for g in range(8):
            far = levels[np.abs(levels - a[p, g]) >= 10]
            a[p, g + 8] = far[np.random.randint(len(far))]
    return np.exp2(a.ravel()).repeat(32)


def f64(x):
    return np.asarray(x).astype(np.float64)


def striped8(idx):
    return np.asarray(idx).reshape(8, -1, 16).transpose(0, 2, 1).reshape(128, -1).astype(np.uint16)


def unstriped8(offs):
    return offs.reshape(8, 16, -1).transpose(0, 2, 1).reshape(8, -1).astype(np.int64)


def pick8(x, idx, run):
    r = np.arange(len(x))
    return x[r[:, None], idx[r % (8 * run) // run]]


E2M1 = np.array([0.0, 0.5, 1.0, 1.5, 2.0, 3.0, 4.0, 6.0, -0.0, -0.5, -1.0, -1.5, -2.0, -3.0, -4.0, -6.0])


def pack_weight(w, fmt):
    k, n = w.shape
    w = f64(np.asarray(w, np.float32).astype(ml_dtypes.bfloat16)).reshape(k // 32, 32, n)
    amax = np.abs(w).max(1)
    if fmt == "e4m3":
        byte = np.frexp(amax)[1] - 1 + 127 - 7
    else:
        mant, ex = np.frexp(amax / 6.0)
        byte = np.where(mant > 0.5, ex, ex - 1) + 127
    byte = np.clip(np.where(amax > 0, byte, 1), 1, 254)
    scaled = (w * np.exp2(127.0 - byte)[:, None, :]).reshape(k, n).astype(np.float32)
    by_word = np.ascontiguousarray(scaled.reshape(k // 512, 128, 4, n).transpose(0, 1, 3, 2))
    if fmt == "e4m3":
        words = by_word.astype(ml_dtypes.float8_e4m3fn).view(np.uint8)
    else:
        c = by_word.astype(ml_dtypes.float4_e2m1fn).view(np.uint8) & 0xF
        words = (c[..., 0::2] | (c[..., 1::2] << 4)).reshape(k // 512, 128, 2 * n)
    return np.ascontiguousarray(words), np.ascontiguousarray(byte.astype(np.uint8).reshape(k // 512, 16, n))


def unpack_weight(words, scales, fmt):
    g, _, n = scales.shape
    words = np.ascontiguousarray(words).reshape(g, 128, n, -1)
    if fmt == "e4m3":
        vals = words.view(ml_dtypes.float8_e4m3fn).astype(np.float64)
    else:
        nib = np.empty((g, 128, n, 4), np.uint8)
        nib[..., 0::2] = words & 0xF
        nib[..., 1::2] = words >> 4
        vals = E2M1[nib]
    vals = vals * np.repeat(np.exp2(scales.astype(np.float64) - 127.0), 8, axis=1)[..., None]
    return vals.transpose(0, 1, 3, 2).reshape(g * 512, n)


D, V, Q, I = 512, 2048, 128, 512


def setup_inputs():
    n = np.random.standard_normal
    idx = np.stack([np.random.permutation(V)[:I] for _ in range(8)])
    fd = mx_kscale(D)
    vocp = pack_weight(n((D, V)) / fd[:, None], "e2m1")
    return {
        "hid": (n((D, Q)) * 1.0 / np.sqrt(D) * fd[:, None]).astype(np.float32),
        "voc_words": vocp[0],
        "voc_scales": vocp[1],
        "fac": (np.random.uniform(300.0, 1500.0, (Q, 1))).astype(np.float32),
        "sw": (np.random.uniform(0.5, 2.0, (1, I))).astype(np.float32),
        "dhid": (n((D, Q)) * 1.0 / np.sqrt(D) * fd[:, None]).astype(np.float32),
        "base": (0.5 * n((Q, V))).astype(np.float32),
        "offs": striped8(idx),
    }


def reference(hid, voc_words, voc_scales, fac, sw, dhid, base, offs):
    idx = unstriped8(offs)
    vocu = unpack_weight(voc_words, voc_scales, "e2m1")
    hidq = mxq(f64(hid), 0, "e4m3")
    a = hidq.T @ vocu
    dhidq = mxq(f64(dhid), 0, "e4m3")
    ta = dhidq.T @ vocu
    m1 = np.max(a, axis=1, keepdims=True)
    p = np.exp(a - m1)
    z = np.sum(p, axis=1, keepdims=True)
    px = np.exp(pick8(a, idx, 16) - m1)
    u1 = px / z * f64(fac) + 1.0
    du1 = f64(sw) * (-1.0) / u1
    dpx = du1 * f64(fac) / z
    dz = np.sum(du1 * f64(fac) * px / np.square(z) * (-1.0), axis=1, keepdims=True)
    xp = ta * p
    xz = np.sum(xp, axis=1, keepdims=True)
    xpx = pick8(ta, idx, 16) * px
    xu1 = (xpx - xz * px / z) / z * f64(fac)
    xdu1 = xu1 * f64(sw) * (-1.0) / np.square(u1) * (-1.0)
    xdpx = (xdu1 * f64(fac) - xz * du1 * f64(fac) / z) / z
    xdz = np.sum((xdu1 * f64(fac) * px + xpx * du1 * f64(fac) - xz * z * 2.0 * du1 * f64(fac) * px / np.square(z)) / np.square(z) * (-1.0), axis=1, keepdims=True)
    xe1 = xdpx * px + xpx * dpx
    xs1 = np.zeros((Q, V))
    xs1[np.arange(Q)[:, None], idx[np.arange(Q) % 128 // 16]] = xe1
    xda = xdz * p + xp * dz + xs1
    y = xda * 64.0 + f64(base)
    return y

@@ -1,0 +1,164 @@
+from contextlib import ExitStack
+
+import concourse.mybir as mybir
+
+F32 = mybir.dt.float32
+BF16 = mybir.dt.bfloat16
+I32 = mybir.dt.int32
+U32 = mybir.dt.uint32
+U16 = mybir.dt.uint16
+U8 = mybir.dt.uint8
+FP8X4 = mybir.dt.float8_e4m3fn_x4
+FP4X4 = mybir.dt.float4_e2m1fn_x4
+ALU = mybir.AluOpType
+ACT = mybir.ActivationFunctionType
+AX = mybir.AxisListType
+
+P = 128
+D, V, Q, I = 512, 2048, 128, 512
+BANK = 512
+NB = V // BANK
+GAIN = 64.0
+FLOPS = 2 * 2 * D * Q * V
+OUT_WIDTHS = (512, 512, 512, 256, 256)
+
+
+def tile_attend_hvdiscouraged_heads_kernel(tc, hid, voc_words, voc_scales, fac, sw, dhid, base, offs, out):
+    nc = tc.nc
+    with ExitStack() as ctx:
+        keep = ctx.enter_context(tc.tile_pool(name="keep", bufs=1))
+        psum = ctx.enter_context(tc.psum_pool(name="psum", bufs=1))
+
+        offsets = keep.tile([P, I // 16], U16, name="offsets")
+        hid_raw = keep.tile([P, 4, Q], F32, name="hid_raw")
+        dhid_raw = keep.tile([P, 4, Q], F32, name="dhid_raw")
+        words = [keep.tile([P, V], U8, name="words%d" % h, align_bytes=64) for h in range(2)]
+        voc_plane = keep.tile([P, V], U8, name="voc_plane", align_bytes=64)
+        fac_sb = keep.tile([P, 1], F32, name="fac_sb")
+        sw_sb = keep.tile([P, I], F32, name="sw_sb")
+        base_sb = keep.tile([P, V], F32, name="base_sb")
+        spread = keep.tile([P, V], F32, name="spread")
+
+        nc.vector.memset(spread[:], 0.0)
+
+        nc.scalar.dma_start(fac_sb[:], fac)
+        fac_gain = keep.tile([P, 1], F32, name="fac_gain")
+        nc.scalar.activation(fac_gain[:], fac_sb[:], ACT.Copy, scale=-GAIN)
+        nc.sync.dma_start(hid_raw[:], hid.rearrange("(p j) q -> p j q", j=4))
+        for g in range(4):
+            nc.sync.dma_start(voc_plane[32 * g : 32 * g + 4, :].bitcast(I32), voc_scales[0, 4 * g : 4 * g + 4, :].bitcast(I32))
+        nc.sync.dma_start(words[0][:].bitcast(I32), voc_words[0, :, 0:V].bitcast(I32))
+        nc.sync.dma_start(dhid_raw[:], dhid.rearrange("(p j) q -> p j q", j=4))
+        nc.sync.dma_start(words[1][:].bitcast(I32), voc_words[0, :, V : 2 * V].bitcast(I32))
+        nc.sync.dma_start(offsets[:], offs)
+        nc.sync.dma_start(sw_sb[:], sw[0].partition_broadcast(P))
+        nc.sync.dma_start(base_sb[:], base)
+
+        hid_bf = keep.tile([P, Q, 4], BF16, name="hid_bf", align_bytes=64)
+        dhid_bf = keep.tile([P, Q, 4], BF16, name="dhid_bf", align_bytes=64)
+        hid_codes = keep.tile([P, Q], U32, name="hid_codes", align_bytes=64)
+        dhid_codes = keep.tile([P, Q], U32, name="dhid_codes", align_bytes=64)
+        hid_plane = keep.tile([P, Q], U8, name="hid_plane", align_bytes=64)
+        dhid_plane = keep.tile([P, Q], U8, name="dhid_plane", align_bytes=64)
+        nc.vector.tensor_copy(hid_bf[:], hid_raw[:].rearrange("p j q -> p q j"))
+        nc.vector.quantize_mx(out=hid_codes[:].bitcast(FP8X4), scales=hid_plane[:], in_=hid_bf[:].rearrange("p q j -> p (q j)"))
+        nc.scalar.activation(dhid_bf[:], dhid_raw[:].rearrange("p j q -> p q j"), ACT.Copy)
+        nc.vector.quantize_mx(out=dhid_codes[:].bitcast(FP8X4), scales=dhid_plane[:], in_=dhid_bf[:].rearrange("p q j -> p (q j)"))
+
+        a_sb = keep.tile([P, V], F32, name="a_sb")
+        ta_sb = keep.tile([P, V], F32, name="ta_sb")
+        bank_max = keep.tile([P, NB], F32, name="bank_max")
+
+        def score(codes, plane, b, name):
+            bank = psum.tile([P, BANK], F32, name=name)
+            lo = 2 * BANK * (b % 2)
+            nc.tensor.matmul_mx(
+                out=bank[:],
+                lhsT=codes[:].bitcast(FP8X4),
+                lhsT_scale=plane[:],
+                rhs=words[b // 2][:, lo : lo + 2 * BANK].bitcast(FP4X4),
+                rhs_scale=voc_plane[:, b * BANK : (b + 1) * BANK],
+                start=True,
+                stop=True,
+            )
+            return bank
+
+        def score_a(b):
+            bank = score(hid_codes, hid_plane, b, "a_bank%d" % b)
+            nc.vector.tensor_scalar(a_sb[:, b * BANK : (b + 1) * BANK], bank[:], 1.0, None, ALU.mult, ALU.max, accum_out=bank_max[:, b : b + 1])
+
+        score_a(0)
+        score_a(1)
+        ta_banks = [score(dhid_codes, dhid_plane, 0, "ta_bank0")]
+        score_a(2)
+        score_a(3)
+        ta_banks.extend(score(dhid_codes, dhid_plane, b, "ta_bank%d" % b) for b in range(1, NB))
+        for b in range(2):
+            nc.scalar.activation(ta_sb[:, b * BANK : (b + 1) * BANK], ta_banks[b][:], ACT.Copy)
+
+        neg_max = keep.tile([P, 1], F32, name="neg_max")
+        nc.vector.tensor_reduce(neg_max[:], bank_max[:], AX.X, ALU.max, negate=True)
+
+        p_sb = keep.tile([P, V], F32, name="p_sb")
+        z = keep.tile([P, 1], F32, name="z")
+        nc.scalar.activation(p_sb[:], a_sb[:], ACT.Exp, bias=neg_max[:], accum_out=z[:])
+
+        a_pick = keep.tile([P, I], F32, name="a_pick")
+        ta_pick = keep.tile([P, I], F32, name="ta_pick")
+        nc.vector.tensor_copy(a_pick[:], a_sb[:].indirect(offsets[:]))
+        for b in range(2, NB):
+            nc.vector.tensor_copy(ta_sb[:, b * BANK : (b + 1) * BANK], ta_banks[b][:])
+        nc.vector.tensor_copy(ta_pick[:], ta_sb[:].indirect(offsets[:]))
+        px = keep.tile([P, I], F32, name="px")
+        nc.scalar.activation(px[:], a_pick[:], ACT.Exp, bias=neg_max[:])
+
+        inv_z = keep.tile([P, 1], F32, name="inv_z")
+        nc.vector.reciprocal(inv_z[:], z[:])
+        c = keep.tile([P, 1], F32, name="c")
+        nc.vector.tensor_scalar(c[:], fac_sb[:], inv_z[:], None, ALU.mult)
+        c_gain = keep.tile([P, 1], F32, name="c_gain")
+        nc.vector.tensor_scalar(c_gain[:], fac_gain[:], inv_z[:], None, ALU.mult)
+
+        u_sq = keep.tile([P, I], F32, name="u_sq")
+        nc.scalar.activation(u_sq[:], px[:], ACT.Square, bias=1.0, scale=c[:])
+        inv_abs = keep.tile([P, I], F32, name="inv_abs")
+        nc.scalar.activation(inv_abs[:], u_sq[:], ACT.Abs_reciprocal_sqrt)
+        inv_sq = keep.tile([P, I], F32, name="inv_sq")
+        nc.scalar.activation(inv_sq[:], inv_abs[:], ACT.Square)
+
+        xp = keep.tile([P, V], F32, name="xp")
+        mu = keep.tile([P, 1], F32, name="mu")
+        nc.vector.scalar_tensor_tensor(xp[:], ta_sb[:], inv_z[:], p_sb[:], ALU.mult, ALU.mult, accum_out=mu[:])
+        w_px = keep.tile([P, I], F32, name="w_px")
+        nc.vector.tensor_tensor(w_px[:], px[:], sw_sb[:], ALU.mult)
+
+        k = keep.tile([P, I], F32, name="k")
+        k_sum = keep.tile([P, 1], F32, name="k_sum")
+        nc.vector.scalar_tensor_tensor(k[:], inv_sq[:], c_gain[:], w_px[:], ALU.mult, ALU.mult, accum_out=k_sum[:])
+        xe = keep.tile([P, I], F32, name="xe")
+        xe_sum = keep.tile([P, 1], F32, name="xe_sum")
+        nc.vector.scalar_tensor_tensor(xe[:], ta_pick[:], mu[:], k[:], ALU.subtract, ALU.mult, accum_out=xe_sum[:])
+        ks = keep.tile([P, I], F32, name="ks")
+        ks_sum = keep.tile([P, 1], F32, name="ks_sum")
+        nc.vector.scalar_tensor_tensor(ks[:], px[:], c[:], k[:], ALU.mult, ALU.mult, accum_out=ks_sum[:])
+
+        nc.vector.tensor_copy(spread[:].indirect(offsets[:]), xe[:])
+
+        neg_g = keep.tile([P, 1], F32, name="neg_g")
+        nc.vector.tensor_scalar(neg_g[:], k_sum[:], ks_sum[:], mu[:], ALU.add, ALU.mult)
+        coef_xp = keep.tile([P, 1], F32, name="coef_xp")
+        nc.vector.tensor_scalar(coef_xp[:], k_sum[:], ks_sum[:], -1.0, ALU.add, ALU.mult)
+        coef_p = keep.tile([P, 1], F32, name="coef_p")
+        nc.vector.tensor_scalar(coef_p[:], neg_g[:], xe_sum[:], inv_z[:], ALU.subtract, ALU.mult)
+
+        lo = 0
+        for n, width in enumerate(OUT_WIDTHS):
+            cols = slice(lo, lo + width)
+            lo = lo + width
+            s1 = keep.tile([P, width], F32, name="s1_%d" % n)
+            s2 = keep.tile([P, width], F32, name="s2_%d" % n)
+            res = keep.tile([P, width], F32, name="res_%d" % n)
+            nc.vector.scalar_tensor_tensor(s1[:], xp[:, cols], coef_xp[:], base_sb[:, cols], ALU.mult, ALU.add)
+            nc.vector.scalar_tensor_tensor(s2[:], p_sb[:, cols], coef_p[:], s1[:], ALU.mult, ALU.add)
+            nc.vector.tensor_tensor(res[:], s2[:], spread[:, cols], ALU.add)
+            nc.sync.dma_start(out[:, cols], res[:])

@@ -1,6 +1,7 @@
 from contextlib import ExitStack
 
 import concourse.mybir as mybir
+from concourse.masks import make_identity
 
 F32 = mybir.dt.float32
 BF16 = mybir.dt.bfloat16
@@ -40,6 +41,8 @@ def tile_attend_hvdiscouraged_heads_kernel(tc, hid, voc_words, voc_scales, fac, 
         spread = keep.tile([P, V], F32, name="spread")
 
         nc.vector.memset(spread[:], 0.0)
+        ident = keep.tile([P, P], F32, name="ident")
+        make_identity(nc, ident[:])
 
         nc.scalar.dma_start(fac_sb[:], fac)
         fac_gain = keep.tile([P, 1], F32, name="fac_gain")
@@ -86,14 +89,11 @@ def tile_attend_hvdiscouraged_heads_kernel(tc, hid, voc_words, voc_scales, fac, 
         def score_a(b):
             bank = score(hid_codes, hid_plane, b, "a_bank%d" % b)
             nc.vector.tensor_scalar(a_sb[:, b * BANK : (b + 1) * BANK], bank[:], 1.0, None, ALU.mult, ALU.max, accum_out=bank_max[:, b : b + 1])
+            return bank
 
-        score_a(0)
-        score_a(1)
-        ta_banks = [score(dhid_codes, dhid_plane, 0, "ta_bank0")]
-        score_a(2)
-        score_a(3)
-        ta_banks.extend(score(dhid_codes, dhid_plane, b, "ta_bank%d" % b) for b in range(1, NB))
-        for b in range(2):
+        a_banks = [score_a(b) for b in range(NB)]
+        ta_banks = [score(dhid_codes, dhid_plane, b, "ta_bank%d" % b) for b in range(NB)]
+        for b in range(1):
             nc.scalar.activation(ta_sb[:, b * BANK : (b + 1) * BANK], ta_banks[b][:], ACT.Copy)
 
         neg_max = keep.tile([P, 1], F32, name="neg_max")
@@ -106,31 +106,43 @@ def tile_attend_hvdiscouraged_heads_kernel(tc, hid, voc_words, voc_scales, fac, 
         a_pick = keep.tile([P, I], F32, name="a_pick")
         ta_pick = keep.tile([P, I], F32, name="ta_pick")
         nc.vector.tensor_copy(a_pick[:], a_sb[:].indirect(offsets[:]))
-        for b in range(2, NB):
+        for b in range(1, NB):
             nc.vector.tensor_copy(ta_sb[:, b * BANK : (b + 1) * BANK], ta_banks[b][:])
         nc.vector.tensor_copy(ta_pick[:], ta_sb[:].indirect(offsets[:]))
         px = keep.tile([P, I], F32, name="px")
         nc.scalar.activation(px[:], a_pick[:], ACT.Exp, bias=neg_max[:])
 
-        inv_z = keep.tile([P, 1], F32, name="inv_z")
-        nc.vector.reciprocal(inv_z[:], z[:])
-        c = keep.tile([P, 1], F32, name="c")
-        nc.vector.tensor_scalar(c[:], fac_sb[:], inv_z[:], None, ALU.mult)
-        c_gain = keep.tile([P, 1], F32, name="c_gain")
-        nc.vector.tensor_scalar(c_gain[:], fac_gain[:], inv_z[:], None, ALU.mult)
-
-        u_sq = keep.tile([P, I], F32, name="u_sq")
-        nc.scalar.activation(u_sq[:], px[:], ACT.Square, bias=1.0, scale=c[:])
+        zu_sq = keep.tile([P, I], F32, name="zu_sq")
+        nc.scalar.activation(zu_sq[:], px[:], ACT.Square, bias=z[:], scale=fac_sb[:])
         inv_abs = keep.tile([P, I], F32, name="inv_abs")
-        nc.scalar.activation(inv_abs[:], u_sq[:], ACT.Abs_reciprocal_sqrt)
+        nc.scalar.activation(inv_abs[:], zu_sq[:], ACT.Abs_reciprocal_sqrt)
         inv_sq = keep.tile([P, I], F32, name="inv_sq")
         nc.scalar.activation(inv_sq[:], inv_abs[:], ACT.Square)
+
+        inv_z = keep.tile([P, 1], F32, name="inv_z")
+        nc.vector.reciprocal(inv_z[:], z[:])
+        c_gain = keep.tile([P, 1], F32, name="c_gain")
+        nc.vector.tensor_scalar(c_gain[:], fac_gain[:], z[:], None, ALU.mult)
+        c = keep.tile([P, 1], F32, name="c")
+        nc.vector.tensor_scalar(c[:], fac_sb[:], inv_z[:], None, ALU.mult)
+        neg_inv_z = keep.tile([P, 1], F32, name="neg_inv_z")
+        nc.vector.tensor_scalar(neg_inv_z[:], inv_z[:], -1.0, None, ALU.mult)
 
         xp = keep.tile([P, V], F32, name="xp")
         mu = keep.tile([P, 1], F32, name="mu")
         nc.vector.scalar_tensor_tensor(xp[:], ta_sb[:], inv_z[:], p_sb[:], ALU.mult, ALU.mult, accum_out=mu[:])
         w_px = keep.tile([P, I], F32, name="w_px")
         nc.vector.tensor_tensor(w_px[:], px[:], sw_sb[:], ALU.mult)
+        mu_z = keep.tile([P, 1], F32, name="mu_z")
+        nc.vector.tensor_scalar(mu_z[:], mu[:], inv_z[:], None, ALU.mult)
+
+        def turn_into(bank, src, first, last):
+            for j in range(4):
+                blk = slice(j * P, (j + 1) * P)
+                nc.tensor.matmul(bank[:, blk], lhsT=src[:, blk], rhs=ident[:], is_transpose=True, start=first and j == 0, stop=last and j == 3)
+
+        for b in range(NB):
+            turn_into(a_banks[b], base_sb[:, b * BANK : (b + 1) * BANK], True, False)
 
         k = keep.tile([P, I], F32, name="k")
         k_sum = keep.tile([P, 1], F32, name="k_sum")
@@ -141,24 +153,44 @@ def tile_attend_hvdiscouraged_heads_kernel(tc, hid, voc_words, voc_scales, fac, 
         ks = keep.tile([P, I], F32, name="ks")
         ks_sum = keep.tile([P, 1], F32, name="ks_sum")
         nc.vector.scalar_tensor_tensor(ks[:], px[:], c[:], k[:], ALU.mult, ALU.mult, accum_out=ks_sum[:])
-
         nc.vector.tensor_copy(spread[:].indirect(offsets[:]), xe[:])
 
-        neg_g = keep.tile([P, 1], F32, name="neg_g")
-        nc.vector.tensor_scalar(neg_g[:], k_sum[:], ks_sum[:], mu[:], ALU.add, ALU.mult)
-        coef_xp = keep.tile([P, 1], F32, name="coef_xp")
-        nc.vector.tensor_scalar(coef_xp[:], k_sum[:], ks_sum[:], -1.0, ALU.add, ALU.mult)
+        k_term = keep.tile([P, 1], F32, name="k_term")
+        nc.scalar.activation(k_term[:], k_sum[:], ACT.Copy, scale=mu_z[:])
+        k_xe_terms = keep.tile([P, 1], F32, name="k_xe_terms")
+        nc.scalar.activation(k_xe_terms[:], xe_sum[:], ACT.Identity, bias=k_term[:], scale=neg_inv_z[:])
         coef_p = keep.tile([P, 1], F32, name="coef_p")
-        nc.vector.tensor_scalar(coef_p[:], neg_g[:], xe_sum[:], inv_z[:], ALU.subtract, ALU.mult)
+        nc.scalar.activation(coef_p[:], ks_sum[:], ACT.Identity, bias=k_xe_terms[:], scale=mu_z[:])
+        neg_g = keep.tile([P, 1], F32, name="neg_g")
+        nc.scalar.activation(neg_g[:], k_sum[:], ACT.Identity, bias=ks_sum[:])
 
+        scaled_p = [keep.tile([P, BANK], F32, name="scaled_p%d" % b) for b in range(NB)]
+        turned = [keep.tile([P, BANK], F32, name="turned%d" % b) for b in range(NB)]
+
+        def scale_p(b):
+            nc.scalar.activation(scaled_p[b][:], p_sb[:, b * BANK : (b + 1) * BANK], ACT.Copy, scale=coef_p[:])
+            turn_into(a_banks[b], scaled_p[b], False, True)
+
+        def turn_back(b):
+            nc.scalar.activation(turned[b][:], a_banks[b][:], ACT.Copy)
+            for j in range(4):
+                blk = slice(j * P, (j + 1) * P)
+                nc.tensor.transpose(ta_banks[b][:, blk], turned[b][:, blk], ident[:])
+
+        scale_p(0)
+        for b in range(1, NB):
+            scale_p(b)
+            turn_back(b - 1)
+        turn_back(NB - 1)
+
+        part = keep.tile([P, V], F32, name="part")
+        for b in range(NB):
+            cols = slice(b * BANK, (b + 1) * BANK)
+            nc.vector.scalar_tensor_tensor(part[:, cols], xp[:, cols], neg_g[:], spread[:, cols], ALU.mult, ALU.subtract)
         lo = 0
         for n, width in enumerate(OUT_WIDTHS):
             cols = slice(lo, lo + width)
-            lo = lo + width
-            s1 = keep.tile([P, width], F32, name="s1_%d" % n)
-            s2 = keep.tile([P, width], F32, name="s2_%d" % n)
             res = keep.tile([P, width], F32, name="res_%d" % n)
-            nc.vector.scalar_tensor_tensor(s1[:], xp[:, cols], coef_xp[:], base_sb[:, cols], ALU.mult, ALU.add)
-            nc.vector.scalar_tensor_tensor(s2[:], p_sb[:, cols], coef_p[:], s1[:], ALU.mult, ALU.add)
-            nc.vector.tensor_tensor(res[:], s2[:], spread[:, cols], ALU.add)
+            nc.vector.tensor_tensor(res[:], ta_banks[lo // BANK][:, lo % BANK : lo % BANK + width], part[:, cols], ALU.subtract)
             nc.sync.dma_start(out[:, cols], res[:])
+            lo = lo + width

@@ -20,8 +20,9 @@ D, V, Q, I = 512, 2048, 128, 512
 BANK = 512
 NB = V // BANK
 GAIN = 64.0
+VECTOR_XP_BANKS = 2
 FLOPS = 2 * 2 * D * Q * V
-OUT_WIDTHS = (512, 512, 512, 256, 256)
+OUT_WIDTHS = (512, 512, 512, 384, 128)
 
 
 def tile_attend_hvdiscouraged_heads_kernel(tc, hid, voc_words, voc_scales, fac, sw, dhid, base, offs, out):
@@ -48,11 +49,11 @@ def tile_attend_hvdiscouraged_heads_kernel(tc, hid, voc_words, voc_scales, fac, 
         fac_gain = keep.tile([P, 1], F32, name="fac_gain")
         nc.scalar.activation(fac_gain[:], fac_sb[:], ACT.Copy, scale=-GAIN)
         nc.sync.dma_start(hid_raw[:], hid.rearrange("(p j) q -> p j q", j=4))
-        for g in range(4):
-            nc.sync.dma_start(voc_plane[32 * g : 32 * g + 4, :].bitcast(I32), voc_scales[0, 4 * g : 4 * g + 4, :].bitcast(I32))
+        for r in range(4):
+            nc.sync.dma_start(voc_plane[r:P:32, :].bitcast(I32), voc_scales[0, r:16:4, :].bitcast(I32))
         nc.sync.dma_start(words[0][:].bitcast(I32), voc_words[0, :, 0:V].bitcast(I32))
-        nc.sync.dma_start(dhid_raw[:], dhid.rearrange("(p j) q -> p j q", j=4))
         nc.sync.dma_start(words[1][:].bitcast(I32), voc_words[0, :, V : 2 * V].bitcast(I32))
+        nc.sync.dma_start(dhid_raw[:], dhid.rearrange("(p j) q -> p j q", j=4))
         nc.sync.dma_start(offsets[:], offs)
         nc.sync.dma_start(sw_sb[:], sw[0].partition_broadcast(P))
         nc.sync.dma_start(base_sb[:], base)
@@ -65,7 +66,7 @@ def tile_attend_hvdiscouraged_heads_kernel(tc, hid, voc_words, voc_scales, fac, 
         dhid_plane = keep.tile([P, Q], U8, name="dhid_plane", align_bytes=64)
         nc.vector.tensor_copy(hid_bf[:], hid_raw[:].rearrange("p j q -> p q j"))
         nc.vector.quantize_mx(out=hid_codes[:].bitcast(FP8X4), scales=hid_plane[:], in_=hid_bf[:].rearrange("p q j -> p (q j)"))
-        nc.scalar.activation(dhid_bf[:], dhid_raw[:].rearrange("p j q -> p q j"), ACT.Copy)
+        nc.scalar.copy(dhid_bf[:], dhid_raw[:].rearrange("p j q -> p q j"))
         nc.vector.quantize_mx(out=dhid_codes[:].bitcast(FP8X4), scales=dhid_plane[:], in_=dhid_bf[:].rearrange("p q j -> p (q j)"))
 
         a_sb = keep.tile([P, V], F32, name="a_sb")
@@ -123,18 +124,18 @@ def tile_attend_hvdiscouraged_heads_kernel(tc, hid, voc_words, voc_scales, fac, 
         nc.vector.reciprocal(inv_z[:], z[:])
         c_gain = keep.tile([P, 1], F32, name="c_gain")
         nc.vector.tensor_scalar(c_gain[:], fac_gain[:], z[:], None, ALU.mult)
-        c = keep.tile([P, 1], F32, name="c")
-        nc.vector.tensor_scalar(c[:], fac_sb[:], inv_z[:], None, ALU.mult)
-        neg_inv_z = keep.tile([P, 1], F32, name="neg_inv_z")
-        nc.vector.tensor_scalar(neg_inv_z[:], inv_z[:], -1.0, None, ALU.mult)
 
         xp = keep.tile([P, V], F32, name="xp")
         mu = keep.tile([P, 1], F32, name="mu")
         nc.vector.scalar_tensor_tensor(xp[:], ta_sb[:], inv_z[:], p_sb[:], ALU.mult, ALU.mult, accum_out=mu[:])
         w_px = keep.tile([P, I], F32, name="w_px")
         nc.vector.tensor_tensor(w_px[:], px[:], sw_sb[:], ALU.mult)
+        c = keep.tile([P, 1], F32, name="c")
+        nc.scalar.activation(c[:], fac_sb[:], ACT.Copy, scale=inv_z[:])
+        neg_inv_z = keep.tile([P, 1], F32, name="neg_inv_z")
+        nc.scalar.activation(neg_inv_z[:], inv_z[:], ACT.Copy, scale=-1.0)
         mu_z = keep.tile([P, 1], F32, name="mu_z")
-        nc.vector.tensor_scalar(mu_z[:], mu[:], inv_z[:], None, ALU.mult)
+        nc.scalar.activation(mu_z[:], mu[:], ACT.Copy, scale=inv_z[:])
 
         def turn_into(bank, src, first, last):
             for j in range(4):
@@ -147,29 +148,31 @@ def tile_attend_hvdiscouraged_heads_kernel(tc, hid, voc_words, voc_scales, fac, 
         k = keep.tile([P, I], F32, name="k")
         k_sum = keep.tile([P, 1], F32, name="k_sum")
         nc.vector.scalar_tensor_tensor(k[:], inv_sq[:], c_gain[:], w_px[:], ALU.mult, ALU.mult, accum_out=k_sum[:])
-        xe = keep.tile([P, I], F32, name="xe")
-        xe_sum = keep.tile([P, 1], F32, name="xe_sum")
-        nc.vector.scalar_tensor_tensor(xe[:], ta_pick[:], mu[:], k[:], ALU.subtract, ALU.mult, accum_out=xe_sum[:])
         ks = keep.tile([P, I], F32, name="ks")
         ks_sum = keep.tile([P, 1], F32, name="ks_sum")
         nc.vector.scalar_tensor_tensor(ks[:], px[:], c[:], k[:], ALU.mult, ALU.mult, accum_out=ks_sum[:])
+        xe = keep.tile([P, I], F32, name="xe")
+        xe_sum = keep.tile([P, 1], F32, name="xe_sum")
+        nc.vector.scalar_tensor_tensor(xe[:], ta_pick[:], mu[:], k[:], ALU.subtract, ALU.mult, accum_out=xe_sum[:])
         nc.vector.tensor_copy(spread[:].indirect(offsets[:]), xe[:])
 
+        neg_k_sum = keep.tile([P, 1], F32, name="neg_k_sum")
+        nc.scalar.activation(neg_k_sum[:], k_sum[:], ACT.Copy, scale=-1.0)
         k_term = keep.tile([P, 1], F32, name="k_term")
         nc.scalar.activation(k_term[:], k_sum[:], ACT.Copy, scale=mu_z[:])
-        k_xe_terms = keep.tile([P, 1], F32, name="k_xe_terms")
-        nc.scalar.activation(k_xe_terms[:], xe_sum[:], ACT.Identity, bias=k_term[:], scale=neg_inv_z[:])
+        coef_xp = keep.tile([P, 1], F32, name="coef_xp")
+        nc.scalar.activation(coef_xp[:], ks_sum[:], ACT.Identity, bias=neg_k_sum[:], scale=-1.0)
+        g_term = keep.tile([P, 1], F32, name="g_term")
+        nc.scalar.activation(g_term[:], ks_sum[:], ACT.Identity, bias=k_term[:], scale=mu_z[:])
         coef_p = keep.tile([P, 1], F32, name="coef_p")
-        nc.scalar.activation(coef_p[:], ks_sum[:], ACT.Identity, bias=k_xe_terms[:], scale=mu_z[:])
-        neg_g = keep.tile([P, 1], F32, name="neg_g")
-        nc.scalar.activation(neg_g[:], k_sum[:], ACT.Identity, bias=ks_sum[:])
+        nc.scalar.activation(coef_p[:], xe_sum[:], ACT.Identity, bias=g_term[:], scale=neg_inv_z[:])
 
-        scaled_p = [keep.tile([P, BANK], F32, name="scaled_p%d" % b) for b in range(NB)]
         turned = [keep.tile([P, BANK], F32, name="turned%d" % b) for b in range(NB)]
 
-        def scale_p(b):
-            nc.scalar.activation(scaled_p[b][:], p_sb[:, b * BANK : (b + 1) * BANK], ACT.Copy, scale=coef_p[:])
-            turn_into(a_banks[b], scaled_p[b], False, True)
+        def add_scaled(b, src, coef, last, name):
+            scaled = keep.tile([P, BANK], F32, name=name)
+            nc.scalar.activation(scaled[:], src[:, b * BANK : (b + 1) * BANK], ACT.Copy, scale=coef[:])
+            turn_into(a_banks[b], scaled, False, last)
 
         def turn_back(b):
             nc.scalar.activation(turned[b][:], a_banks[b][:], ACT.Copy)
@@ -177,20 +180,24 @@ def tile_attend_hvdiscouraged_heads_kernel(tc, hid, voc_words, voc_scales, fac, 
                 blk = slice(j * P, (j + 1) * P)
                 nc.tensor.transpose(ta_banks[b][:, blk], turned[b][:, blk], ident[:])
 
-        scale_p(0)
-        for b in range(1, NB):
-            scale_p(b)
-            turn_back(b - 1)
+        for b in range(VECTOR_XP_BANKS, NB):
+            add_scaled(b, xp, coef_xp, False, "scaled_xp%d" % b)
+        for b in range(NB):
+            add_scaled(b, p_sb, coef_p, True, "scaled_p%d" % b)
+            if b >= 2:
+                turn_back(b - 2)
+        turn_back(NB - 2)
         turn_back(NB - 1)
 
-        part = keep.tile([P, V], F32, name="part")
-        for b in range(NB):
+        part = keep.tile([P, VECTOR_XP_BANKS * BANK], F32, name="part")
+        for b in range(VECTOR_XP_BANKS):
             cols = slice(b * BANK, (b + 1) * BANK)
-            nc.vector.scalar_tensor_tensor(part[:, cols], xp[:, cols], neg_g[:], spread[:, cols], ALU.mult, ALU.subtract)
+            nc.vector.scalar_tensor_tensor(part[:, cols], xp[:, cols], coef_xp[:], spread[:, cols], ALU.mult, ALU.add)
         lo = 0
         for n, width in enumerate(OUT_WIDTHS):
             cols = slice(lo, lo + width)
             res = keep.tile([P, width], F32, name="res_%d" % n)
-            nc.vector.tensor_tensor(res[:], ta_banks[lo // BANK][:, lo % BANK : lo % BANK + width], part[:, cols], ALU.subtract)
+            other = part if lo < VECTOR_XP_BANKS * BANK else spread
+            nc.vector.tensor_tensor(res[:], ta_banks[lo // BANK][:, lo % BANK : lo % BANK + width], other[:, cols], ALU.add)
             nc.sync.dma_start(out[:, cols], res[:])
             lo = lo + width

from contextlib import ExitStack

import concourse.mybir as mybir
from concourse.masks import make_identity

F32 = mybir.dt.float32
BF16 = mybir.dt.bfloat16
I32 = mybir.dt.int32
U32 = mybir.dt.uint32
U16 = mybir.dt.uint16
U8 = mybir.dt.uint8
FP8X4 = mybir.dt.float8_e4m3fn_x4
FP4X4 = mybir.dt.float4_e2m1fn_x4
ALU = mybir.AluOpType
ACT = mybir.ActivationFunctionType
AX = mybir.AxisListType

P = 128
D, V, Q, I = 512, 2048, 128, 512
BANK = 512
NB = V // BANK
GAIN = 64.0
VECTOR_XP_BANKS = 2
FLOPS = 2 * 2 * D * Q * V
OUT_WIDTHS = (512, 512, 512, 384, 128)


def tile_attend_hvdiscouraged_heads_kernel(tc, hid, voc_words, voc_scales, fac, sw, dhid, base, offs, out):
    nc = tc.nc
    with ExitStack() as ctx:
        keep = ctx.enter_context(tc.tile_pool(name="keep", bufs=1))
        psum = ctx.enter_context(tc.psum_pool(name="psum", bufs=1))

        offsets = keep.tile([P, I // 16], U16, name="offsets")
        hid_raw = keep.tile([P, 4, Q], F32, name="hid_raw")
        dhid_raw = keep.tile([P, 4, Q], F32, name="dhid_raw")
        words = [keep.tile([P, V], U8, name="words%d" % h, align_bytes=64) for h in range(2)]
        voc_plane = keep.tile([P, V], U8, name="voc_plane", align_bytes=64)
        fac_sb = keep.tile([P, 1], F32, name="fac_sb")
        sw_sb = keep.tile([P, I], F32, name="sw_sb")
        base_sb = keep.tile([P, V], F32, name="base_sb")
        spread = keep.tile([P, V], F32, name="spread")

        nc.vector.memset(spread[:], 0.0)
        ident = keep.tile([P, P], F32, name="ident")
        make_identity(nc, ident[:])

        nc.scalar.dma_start(fac_sb[:], fac)
        fac_gain = keep.tile([P, 1], F32, name="fac_gain")
        nc.scalar.activation(fac_gain[:], fac_sb[:], ACT.Copy, scale=-GAIN)
        nc.sync.dma_start(hid_raw[:], hid.rearrange("(p j) q -> p j q", j=4))
        for r in range(4):
            nc.sync.dma_start(voc_plane[r:P:32, :].bitcast(I32), voc_scales[0, r:16:4, :].bitcast(I32))
        nc.sync.dma_start(words[0][:].bitcast(I32), voc_words[0, :, 0:V].bitcast(I32))
        nc.sync.dma_start(words[1][:].bitcast(I32), voc_words[0, :, V : 2 * V].bitcast(I32))
        nc.sync.dma_start(dhid_raw[:], dhid.rearrange("(p j) q -> p j q", j=4))
        nc.sync.dma_start(offsets[:], offs)
        nc.sync.dma_start(sw_sb[:], sw[0].partition_broadcast(P))
        nc.sync.dma_start(base_sb[:], base)

        hid_bf = keep.tile([P, Q, 4], BF16, name="hid_bf", align_bytes=64)
        dhid_bf = keep.tile([P, Q, 4], BF16, name="dhid_bf", align_bytes=64)
        hid_codes = keep.tile([P, Q], U32, name="hid_codes", align_bytes=64)
        dhid_codes = keep.tile([P, Q], U32, name="dhid_codes", align_bytes=64)
        hid_plane = keep.tile([P, Q], U8, name="hid_plane", align_bytes=64)
        dhid_plane = keep.tile([P, Q], U8, name="dhid_plane", align_bytes=64)
        nc.vector.tensor_copy(hid_bf[:], hid_raw[:].rearrange("p j q -> p q j"))
        nc.vector.quantize_mx(out=hid_codes[:].bitcast(FP8X4), scales=hid_plane[:], in_=hid_bf[:].rearrange("p q j -> p (q j)"))
        nc.scalar.copy(dhid_bf[:], dhid_raw[:].rearrange("p j q -> p q j"))
        nc.vector.quantize_mx(out=dhid_codes[:].bitcast(FP8X4), scales=dhid_plane[:], in_=dhid_bf[:].rearrange("p q j -> p (q j)"))

        a_sb = keep.tile([P, V], F32, name="a_sb")
        ta_sb = keep.tile([P, V], F32, name="ta_sb")
        bank_max = keep.tile([P, NB], F32, name="bank_max")

        def score(codes, plane, b, name):
            bank = psum.tile([P, BANK], F32, name=name)
            lo = 2 * BANK * (b % 2)
            nc.tensor.matmul_mx(
                out=bank[:],
                lhsT=codes[:].bitcast(FP8X4),
                lhsT_scale=plane[:],
                rhs=words[b // 2][:, lo : lo + 2 * BANK].bitcast(FP4X4),
                rhs_scale=voc_plane[:, b * BANK : (b + 1) * BANK],
                start=True,
                stop=True,
            )
            return bank

        def score_a(b):
            bank = score(hid_codes, hid_plane, b, "a_bank%d" % b)
            nc.vector.tensor_scalar(a_sb[:, b * BANK : (b + 1) * BANK], bank[:], 1.0, None, ALU.mult, ALU.max, accum_out=bank_max[:, b : b + 1])
            return bank

        a_banks = [score_a(b) for b in range(NB)]
        ta_banks = [score(dhid_codes, dhid_plane, b, "ta_bank%d" % b) for b in range(NB)]
        for b in range(1):
            nc.scalar.activation(ta_sb[:, b * BANK : (b + 1) * BANK], ta_banks[b][:], ACT.Copy)

        neg_max = keep.tile([P, 1], F32, name="neg_max")
        nc.vector.tensor_reduce(neg_max[:], bank_max[:], AX.X, ALU.max, negate=True)

        p_sb = keep.tile([P, V], F32, name="p_sb")
        z = keep.tile([P, 1], F32, name="z")
        nc.scalar.activation(p_sb[:], a_sb[:], ACT.Exp, bias=neg_max[:], accum_out=z[:])

        a_pick = keep.tile([P, I], F32, name="a_pick")
        ta_pick = keep.tile([P, I], F32, name="ta_pick")
        nc.vector.tensor_copy(a_pick[:], a_sb[:].indirect(offsets[:]))
        for b in range(1, NB):
            nc.vector.tensor_copy(ta_sb[:, b * BANK : (b + 1) * BANK], ta_banks[b][:])
        nc.vector.tensor_copy(ta_pick[:], ta_sb[:].indirect(offsets[:]))
        px = keep.tile([P, I], F32, name="px")
        nc.scalar.activation(px[:], a_pick[:], ACT.Exp, bias=neg_max[:])

        zu_sq = keep.tile([P, I], F32, name="zu_sq")
        nc.scalar.activation(zu_sq[:], px[:], ACT.Square, bias=z[:], scale=fac_sb[:])
        inv_abs = keep.tile([P, I], F32, name="inv_abs")
        nc.scalar.activation(inv_abs[:], zu_sq[:], ACT.Abs_reciprocal_sqrt)
        inv_sq = keep.tile([P, I], F32, name="inv_sq")
        nc.scalar.activation(inv_sq[:], inv_abs[:], ACT.Square)

        inv_z = keep.tile([P, 1], F32, name="inv_z")
        nc.vector.reciprocal(inv_z[:], z[:])
        c_gain = keep.tile([P, 1], F32, name="c_gain")
        nc.vector.tensor_scalar(c_gain[:], fac_gain[:], z[:], None, ALU.mult)

        xp = keep.tile([P, V], F32, name="xp")
        mu = keep.tile([P, 1], F32, name="mu")
        nc.vector.scalar_tensor_tensor(xp[:], ta_sb[:], inv_z[:], p_sb[:], ALU.mult, ALU.mult, accum_out=mu[:])
        w_px = keep.tile([P, I], F32, name="w_px")
        nc.vector.tensor_tensor(w_px[:], px[:], sw_sb[:], ALU.mult)
        c = keep.tile([P, 1], F32, name="c")
        nc.scalar.activation(c[:], fac_sb[:], ACT.Copy, scale=inv_z[:])
        neg_inv_z = keep.tile([P, 1], F32, name="neg_inv_z")
        nc.scalar.activation(neg_inv_z[:], inv_z[:], ACT.Copy, scale=-1.0)
        mu_z = keep.tile([P, 1], F32, name="mu_z")
        nc.scalar.activation(mu_z[:], mu[:], ACT.Copy, scale=inv_z[:])

        def turn_into(bank, src, first, last):
            for j in range(4):
                blk = slice(j * P, (j + 1) * P)
                nc.tensor.matmul(bank[:, blk], lhsT=src[:, blk], rhs=ident[:], is_transpose=True, start=first and j == 0, stop=last and j == 3)

        for b in range(NB):
            turn_into(a_banks[b], base_sb[:, b * BANK : (b + 1) * BANK], True, False)

        k = keep.tile([P, I], F32, name="k")
        k_sum = keep.tile([P, 1], F32, name="k_sum")
        nc.vector.scalar_tensor_tensor(k[:], inv_sq[:], c_gain[:], w_px[:], ALU.mult, ALU.mult, accum_out=k_sum[:])
        ks = keep.tile([P, I], F32, name="ks")
        ks_sum = keep.tile([P, 1], F32, name="ks_sum")
        nc.vector.scalar_tensor_tensor(ks[:], px[:], c[:], k[:], ALU.mult, ALU.mult, accum_out=ks_sum[:])
        xe = keep.tile([P, I], F32, name="xe")
        xe_sum = keep.tile([P, 1], F32, name="xe_sum")
        nc.vector.scalar_tensor_tensor(xe[:], ta_pick[:], mu[:], k[:], ALU.subtract, ALU.mult, accum_out=xe_sum[:])
        nc.vector.tensor_copy(spread[:].indirect(offsets[:]), xe[:])

        neg_k_sum = keep.tile([P, 1], F32, name="neg_k_sum")
        nc.scalar.activation(neg_k_sum[:], k_sum[:], ACT.Copy, scale=-1.0)
        k_term = keep.tile([P, 1], F32, name="k_term")
        nc.scalar.activation(k_term[:], k_sum[:], ACT.Copy, scale=mu_z[:])
        coef_xp = keep.tile([P, 1], F32, name="coef_xp")
        nc.scalar.activation(coef_xp[:], ks_sum[:], ACT.Identity, bias=neg_k_sum[:], scale=-1.0)
        g_term = keep.tile([P, 1], F32, name="g_term")
        nc.scalar.activation(g_term[:], ks_sum[:], ACT.Identity, bias=k_term[:], scale=mu_z[:])
        coef_p = keep.tile([P, 1], F32, name="coef_p")
        nc.scalar.activation(coef_p[:], xe_sum[:], ACT.Identity, bias=g_term[:], scale=neg_inv_z[:])

        turned = [keep.tile([P, BANK], F32, name="turned%d" % b) for b in range(NB)]

        def add_scaled(b, src, coef, last, name):
            scaled = keep.tile([P, BANK], F32, name=name)
            nc.scalar.activation(scaled[:], src[:, b * BANK : (b + 1) * BANK], ACT.Copy, scale=coef[:])
            turn_into(a_banks[b], scaled, False, last)

        def turn_back(b):
            nc.scalar.activation(turned[b][:], a_banks[b][:], ACT.Copy)
            for j in range(4):
                blk = slice(j * P, (j + 1) * P)
                nc.tensor.transpose(ta_banks[b][:, blk], turned[b][:, blk], ident[:])

        for b in range(VECTOR_XP_BANKS, NB):
            add_scaled(b, xp, coef_xp, False, "scaled_xp%d" % b)
        for b in range(NB):
            add_scaled(b, p_sb, coef_p, True, "scaled_p%d" % b)
            if b >= 2:
                turn_back(b - 2)
        turn_back(NB - 2)
        turn_back(NB - 1)

        part = keep.tile([P, VECTOR_XP_BANKS * BANK], F32, name="part")
        for b in range(VECTOR_XP_BANKS):
            cols = slice(b * BANK, (b + 1) * BANK)
            nc.vector.scalar_tensor_tensor(part[:, cols], xp[:, cols], coef_xp[:], spread[:, cols], ALU.mult, ALU.add)
        lo = 0
        for n, width in enumerate(OUT_WIDTHS):
            cols = slice(lo, lo + width)
            res = keep.tile([P, width], F32, name="res_%d" % n)
            other = part if lo < VECTOR_XP_BANKS * BANK else spread
            nc.vector.tensor_tensor(res[:], ta_banks[lo // BANK][:, lo % BANK : lo % BANK + width], other[:, cols], ALU.add)
            nc.sync.dma_start(out[:, cols], res[:])
            lo = lo + width
